import numpy as np
CORES = [16,17,18,19,20,21,22,23,184,185,186,187,188,189,190,191]
N = 16
ROUNDS = 4
def setup_inputs(rng):
    return {"x": rng.standard_normal((N, ROUNDS, 128, 256), dtype=np.float32)}
def reference(x):
    b = 256 // N
    blocks = x.reshape(N, ROUNDS, 128, N, b)
    return {"y": np.ascontiguousarray(blocks.transpose(3, 1, 2, 0, 4)).reshape(N, ROUNDS, 128, 256)}

@@ -1,0 +1,148 @@
+from concourse.bass import DstId, RemoteDMATransfer
+
+SCRATCH = {
+    "buf": ("sbuf", [128, 24, 2, 16], "float32"),
+}
+SEMAPHORES = ["dma", "a", "b", "c"]
+
+
+def rank_program(g, core, T, topo):
+    rank = T.rank_of(core)
+    if rank is None:
+        return
+    cores = T.cores
+    buf, sem = T.buf, T.sem
+    side, me = rank // 8, rank % 8
+    mine = [cores[side * 8 + i] for i in range(8)]
+    theirs = [cores[(1 - side) * 8 + i] for i in range(8)]
+
+    def is_gw(i):
+        return topo.may_write(mine[i], theirs[0])
+
+    def gw_of(i):
+        leaves = [j for j in range(8) if not is_gw(j) and topo.die(mine[j]) == topo.die(mine[i])]
+        gws = [j for j in range(8) if is_gw(j) and topo.die(mine[j]) == topo.die(mine[i])]
+        return gws[leaves.index(i)]
+
+    def areas(s, i, gen):
+        if gen == 0 or is_gw(i):
+            return (0, 8, 16) if s == 0 else (16, 8, 0)
+        return (8, 16, 0) if s == 0 else (8, 0, 16)
+
+    def dst(d):
+        rid, pid = topo.addr(d, core)
+        return DstId(rid=rid, pnc=pid)
+
+    cnt = {"dma": 0, "a": 0, "b": 0, "c": 0}
+    handle = {"dma": sem.dma, "a": sem.a, "b": sem.b, "c": sem.c}
+
+    def expect(name, n):
+        cnt[name] += n
+
+    def wait(name):
+        g.wait_ge(handle[name], cnt[name])
+
+    def local(out, in_):
+        g.dma_start(out, in_).then_inc(sem.dma, 16)
+        expect("dma", 16)
+
+    def stage(gen, half, st):
+        for k in range(2):
+            local(buf[:, st:st + 8, k, :], T.x[2 * gen + k][:, half * 128:(half + 1) * 128])
+        wait("dma")
+
+    def store(gen):
+        on, cr, _ = areas(side, me, gen)
+        lo = min(on, cr)
+        for k in range(2):
+            local(T.y[2 * gen + k], buf[:, lo:lo + 16, k, :])
+        wait("dma")
+
+    def send_chip(gen, st, peers, rsem, lsem):
+        tr = []
+        for n, p in enumerate(peers):
+            tr.append(RemoteDMATransfer(dst_ids=[dst(mine[p])], dma_engine_mask=3 << (2 * n), remote_sem=handle[rsem],
+                                        src=buf[:, st + p, :, :], dst=buf[:, areas(side, p, gen)[0] + me, :, :]))
+        g.remote_dma_fused(tr, local_sem=handle[lsem])
+        expect(lsem, 2 * len(peers))
+
+    def send_cross(gen, st, source, rsem, lsem):
+        tr = []
+        for d in range(8):
+            tr.append(RemoteDMATransfer(dst_ids=[dst(theirs[d])], dma_engine_mask=1 << d, remote_sem=handle[rsem],
+                                        src=buf[:, st + d, :, :], dst=buf[:, areas(1 - side, d, gen)[1] + source, :, :]))
+        g.remote_dma_fused(tr, local_sem=handle[lsem])
+        expect(lsem, 8)
+
+    def go_ahead(targets, lsem):
+        tr = [RemoteDMATransfer(dst_ids=[dst(d)], dma_engine_mask=1 << n, remote_sem=sem.c) for n, d in enumerate(targets)]
+        g.remote_dma_fused(tr, local_sem=handle[lsem])
+        expect(lsem, len(targets))
+
+    others = [p for p in range(8) if p != me]
+    ARRIVALS = 7 * 2 + 8 * 1
+    own = slice(rank * 16, rank * 16 + 16)
+    local(buf[:, areas(side, me, 0)[0] + me, :, :], T.x[0][:, 0:32])
+
+    if not is_gw(me):
+        gw = gw_of(me)
+        zg = areas(side, gw, 0)[2]
+        rid, pid = topo.addr(mine[gw], core)
+
+        def hand_over(st, lsem):
+            g.remote_dma(buf[:, zg:zg + 8, :, :], buf[:, st:st + 8, :, :], sem.c, handle[lsem], pid, rid, 0xFFFF)
+            expect(lsem, 16)
+
+        z = areas(side, me, 0)[2]
+        stage(0, side, z)
+        send_chip(0, z, others, "a", "b")
+        wait("b")
+        stage(0, 1 - side, z)
+        hand_over(z, "a")
+        expect("a", ARRIVALS)
+        wait("a")
+        store(0)
+        go_ahead([mine[p] for p in others], "a")
+        st = areas(side, me, 1)[2]
+        stage(1, 1 - side, st)
+        hand_over(st, "a")
+        wait("a")
+        stage(1, side, st)
+        expect("c", 7)
+        wait("c")
+        send_chip(1, st, others, "b", "a")
+    else:
+        leaf = [j for j in range(8) if not is_gw(j) and gw_of(j) == me][0]
+        z = areas(side, me, 0)[2]
+        rest = [p for p in others if p != leaf]
+        expect("c", 16)
+        wait("c")
+        send_cross(0, z, leaf, "a", "b")
+        wait("b")
+        stage(0, 1 - side, z)
+        send_cross(0, z, me, "a", "b")
+        wait("b")
+        stage(0, side, z)
+        send_chip(0, z, rest, "a", "b")
+        wait("b")
+        send_chip(0, z, [leaf], "a", "a")
+        expect("a", ARRIVALS)
+        wait("a")
+        store(0)
+        go_ahead([theirs[d] for d in range(8) if is_gw(d)] + [mine[p] for p in others], "a")
+        expect("c", 16 + 7 + 4)
+        wait("c")
+        send_cross(1, z, leaf, "b", "a")
+        wait("a")
+        stage(1, 1 - side, z)
+        send_cross(1, z, me, "b", "a")
+        wait("a")
+        stage(1, side, z)
+        send_chip(1, z, others, "b", "a")
+
+    expect("b", ARRIVALS)
+    wait("b")
+    store(1)
+    local(T.y[:, :, own], T.x[:, :, own])
+    wait("dma")
+    wait("a")

@@ -1,9 +1,13 @@
 from concourse.bass import DstId, RemoteDMATransfer
 
 SCRATCH = {
-    "buf": ("sbuf", [128, 24, 2, 16], "float32"),
+    "buf": ("sbuf", [128, 3, 256], "float32"),
 }
 SEMAPHORES = ["dma", "a", "b", "c"]
+
+SEND_FROM = {True: (0, 1, 0, 1), False: (0, 2, 1, 0)}
+RECEIVE_IN = {True: (1, 0, 1, 0), False: (1, 0, 2, 1)}
+BLK = 16
 
 
 def rank_program(g, core, T, topo):
@@ -24,125 +28,126 @@ def rank_program(g, core, T, topo):
         gws = [j for j in range(8) if is_gw(j) and topo.die(mine[j]) == topo.die(mine[i])]
         return gws[leaves.index(i)]
 
-    def areas(s, i, gen):
-        if gen == 0 or is_gw(i):
-            return (0, 8, 16) if s == 0 else (16, 8, 0)
-        return (8, 16, 0) if s == 0 else (8, 0, 16)
-
-    def dst(d):
-        rid, pid = topo.addr(d, core)
-        return DstId(rid=rid, pnc=pid)
-
+    gateway = is_gw(me)
+    others = [p for p in range(8) if p != me]
     cnt = {"dma": 0, "a": 0, "b": 0, "c": 0}
     handle = {"dma": sem.dma, "a": sem.a, "b": sem.b, "c": sem.c}
 
-    def expect(name, n):
-        cnt[name] += n
-
-    def wait(name):
+    def wait(name, arrivals=0):
+        cnt[name] += arrivals
         g.wait_ge(handle[name], cnt[name])
 
     def local(out, in_):
         g.dma_start(out, in_).then_inc(sem.dma, 16)
-        expect("dma", 16)
+        cnt["dma"] += 16
 
-    def stage(gen, half, st):
-        for k in range(2):
-            local(buf[:, st:st + 8, k, :], T.x[2 * gen + k][:, half * 128:(half + 1) * 128])
-        wait("dma")
+    def slot(b, j):
+        return buf[:, b, j * BLK:(j + 1) * BLK]
 
-    def store(gen):
-        on, cr, _ = areas(side, me, gen)
-        lo = min(on, cr)
-        for k in range(2):
-            local(T.y[2 * gen + k], buf[:, lo:lo + 16, k, :])
-        wait("dma")
+    def transfer(d, mask, rsem, src, dst):
+        rid, pid = topo.addr(d, core)
+        return RemoteDMATransfer(dst_ids=[DstId(rid=rid, pnc=pid)], dma_engine_mask=mask, remote_sem=handle[rsem],
+                                 src=src, dst=dst)
 
-    def send_chip(gen, st, peers, rsem, lsem):
-        tr = []
-        for n, p in enumerate(peers):
-            tr.append(RemoteDMATransfer(dst_ids=[dst(mine[p])], dma_engine_mask=3 << (2 * n), remote_sem=handle[rsem],
-                                        src=buf[:, st + p, :, :], dst=buf[:, areas(side, p, gen)[0] + me, :, :]))
-        g.remote_dma_fused(tr, local_sem=handle[lsem])
-        expect(lsem, 2 * len(peers))
+    def issue(transfers, lsem):
+        g.remote_dma_fused([t for t, _ in transfers], local_sem=handle[lsem])
+        cnt[lsem] += sum(n for _, n in transfers)
 
-    def send_cross(gen, st, source, rsem, lsem):
-        tr = []
-        for d in range(8):
-            tr.append(RemoteDMATransfer(dst_ids=[dst(theirs[d])], dma_engine_mask=1 << d, remote_sem=handle[rsem],
-                                        src=buf[:, st + d, :, :], dst=buf[:, areas(1 - side, d, gen)[1] + source, :, :]))
-        g.remote_dma_fused(tr, local_sem=handle[lsem])
-        expect(lsem, 8)
+    def chip(k, rsem):
+        out = []
+        for n, p in enumerate(others):
+            mask, e = ((1 << (8 + n)), 1) if gateway else ((3 << (2 * n)), 2)
+            out.append((transfer(mine[p], mask, rsem, slot(SEND_FROM[gateway][k], side * 8 + p),
+                                 slot(RECEIVE_IN[is_gw(p)][k], rank)), e))
+        return out
 
-    def go_ahead(targets, lsem):
-        tr = [RemoteDMATransfer(dst_ids=[dst(d)], dma_engine_mask=1 << n, remote_sem=sem.c) for n, d in enumerate(targets)]
-        g.remote_dma_fused(tr, local_sem=handle[lsem])
-        expect(lsem, len(targets))
+    def cross(k, source, src_of, rsem):
+        return [(transfer(theirs[d], 1 << d, rsem, src_of(d), slot(RECEIVE_IN[is_gw(d)][k], side * 8 + source)), 1)
+                for d in range(8)]
 
-    others = [p for p in range(8) if p != me]
-    ARRIVALS = 7 * 2 + 8 * 1
-    own = slice(rank * 16, rank * 16 + 16)
-    local(buf[:, areas(side, me, 0)[0] + me, :, :], T.x[0][:, 0:32])
+    CHIP_IN = sum(1 if is_gw(p) else 2 for p in others)
+    DIRECT_IN = CHIP_IN + 4
+    ROUND_IN = DIRECT_IN + 4
+    xlo = (1 - side) * 128
+    own = slice(rank * BLK, (rank + 1) * BLK)
 
-    if not is_gw(me):
-        gw = gw_of(me)
-        zg = areas(side, gw, 0)[2]
-        rid, pid = topo.addr(mine[gw], core)
+    def load(k):
+        local(buf[:, SEND_FROM[gateway][k], :], T.x[k])
 
-        def hand_over(st, lsem):
-            g.remote_dma(buf[:, zg:zg + 8, :, :], buf[:, st:st + 8, :, :], sem.c, handle[lsem], pid, rid, 0xFFFF)
-            expect(lsem, 16)
+    def store(k):
+        local(T.y[k], buf[:, RECEIVE_IN[gateway][k], :])
 
-        z = areas(side, me, 0)[2]
-        stage(0, side, z)
-        send_chip(0, z, others, "a", "b")
-        wait("b")
-        stage(0, 1 - side, z)
-        hand_over(z, "a")
-        expect("a", ARRIVALS)
-        wait("a")
-        store(0)
-        go_ahead([mine[p] for p in others], "a")
-        st = areas(side, me, 1)[2]
-        stage(1, 1 - side, st)
-        hand_over(st, "a")
-        wait("a")
-        stage(1, side, st)
-        expect("c", 7)
-        wait("c")
-        send_chip(1, st, others, "b", "a")
-    else:
+    local(slot(RECEIVE_IN[gateway][0], rank), T.x[0][:, own])
+    load(0)
+
+    if gateway:
         leaf = [j for j in range(8) if not is_gw(j) and gw_of(j) == me][0]
-        z = areas(side, me, 0)[2]
-        rest = [p for p in others if p != leaf]
-        expect("c", 16)
-        wait("c")
-        send_cross(0, z, leaf, "a", "b")
-        wait("b")
-        stage(0, 1 - side, z)
-        send_cross(0, z, me, "a", "b")
-        wait("b")
-        stage(0, side, z)
-        send_chip(0, z, rest, "a", "b")
-        wait("b")
-        send_chip(0, z, [leaf], "a", "a")
-        expect("a", ARRIVALS)
-        wait("a")
-        store(0)
-        go_ahead([theirs[d] for d in range(8) if is_gw(d)] + [mine[p] for p in others], "a")
-        expect("c", 16 + 7 + 4)
-        wait("c")
-        send_cross(1, z, leaf, "b", "a")
-        wait("a")
-        stage(1, 1 - side, z)
-        send_cross(1, z, me, "b", "a")
-        wait("a")
-        stage(1, side, z)
-        send_chip(1, z, others, "b", "a")
 
-    expect("b", ARRIVALS)
-    wait("b")
-    store(1)
-    local(T.y[:, :, own], T.x[:, :, own])
+        def mine_of(k):
+            return lambda d: slot(SEND_FROM[True][k], (1 - side) * 8 + d)
+
+        def held(k):
+            return lambda d: slot(2, (k % 2) * 8 + d)
+
+        wait("dma")
+        issue(cross(0, me, mine_of(0), "a") + chip(0, "a"), "c")
+        wait("c", 8 + 8)
+        issue(cross(0, leaf, held(0), "a"), "a")
+        wait("a", ROUND_IN)
+        store(0)
+        wait("dma")
+        load(1)
+        wait("dma")
+        issue(cross(1, me, mine_of(1), "b") + chip(1, "b"), "b")
+        issue(cross(1, leaf, held(1), "b"), "b")
+        wait("b", ROUND_IN)
+        store(1)
+        wait("dma")
+        load(2)
+        wait("dma")
+        issue(cross(2, me, mine_of(2), "c") + chip(2, "c"), "c")
+        wait("c", 16 + DIRECT_IN)
+        issue(cross(2, leaf, held(2), "a"), "a")
+        wait("a", 4 + 16)
+        store(2)
+        wait("dma")
+        load(3)
+        wait("dma")
+        issue(cross(3, me, mine_of(3), "b") + chip(3, "b"), "b")
+        issue(cross(3, leaf, held(3), "b"), "b")
+        wait("b", ROUND_IN)
+    else:
+        gw = mine[gw_of(me)]
+
+        def hand_over(k, mask, n, rsem):
+            return [(transfer(gw, mask, rsem, buf[:, SEND_FROM[False][k], xlo:xlo + 128],
+                              buf[:, 2, (k % 2) * 128:(k % 2) * 128 + 128]), n)]
+
+        load(1)
+        wait("dma")
+        issue(chip(0, "a"), "a")
+        issue(hand_over(0, 0x00FF, 8, "c") + hand_over(1, 0xFF00, 8, "c"), "a")
+        wait("a", ROUND_IN)
+        issue(chip(1, "b"), "b")
+        store(0)
+        wait("dma")
+        load(2)
+        wait("b", ROUND_IN)
+        wait("dma")
+        issue(chip(2, "c"), "c")
+        issue(hand_over(2, 0xFFFF, 16, "c"), "c")
+        store(1)
+        wait("dma")
+        load(3)
+        wait("c", DIRECT_IN)
+        wait("dma")
+        issue(hand_over(3, 0xFFFF, 16, "a"), "a")
+        issue(chip(3, "b"), "a")
+        wait("a", 4)
+        store(2)
+        wait("b", ROUND_IN)
+
+    store(3)
     wait("dma")
-    wait("a")
+    local(T.y[1:4, :, own], T.x[1:4, :, own])
+    wait("dma")

from concourse.bass import DstId, RemoteDMATransfer

SCRATCH = {
    "buf": ("sbuf", [128, 3, 256], "float32"),
}
SEMAPHORES = ["dma", "a", "b", "c"]

SEND_FROM = {True: (0, 1, 0, 1), False: (0, 2, 1, 0)}
RECEIVE_IN = {True: (1, 0, 1, 0), False: (1, 0, 2, 1)}
BLK = 16


def rank_program(g, core, T, topo):
    rank = T.rank_of(core)
    if rank is None:
        return
    cores = T.cores
    buf, sem = T.buf, T.sem
    side, me = rank // 8, rank % 8
    mine = [cores[side * 8 + i] for i in range(8)]
    theirs = [cores[(1 - side) * 8 + i] for i in range(8)]

    def is_gw(i):
        return topo.may_write(mine[i], theirs[0])

    def gw_of(i):
        leaves = [j for j in range(8) if not is_gw(j) and topo.die(mine[j]) == topo.die(mine[i])]
        gws = [j for j in range(8) if is_gw(j) and topo.die(mine[j]) == topo.die(mine[i])]
        return gws[leaves.index(i)]

    gateway = is_gw(me)
    others = [p for p in range(8) if p != me]
    cnt = {"dma": 0, "a": 0, "b": 0, "c": 0}
    handle = {"dma": sem.dma, "a": sem.a, "b": sem.b, "c": sem.c}

    def wait(name, arrivals=0):
        cnt[name] += arrivals
        g.wait_ge(handle[name], cnt[name])

    def local(out, in_):
        g.dma_start(out, in_).then_inc(sem.dma, 16)
        cnt["dma"] += 16

    def slot(b, j):
        return buf[:, b, j * BLK:(j + 1) * BLK]

    def transfer(d, mask, rsem, src, dst):
        rid, pid = topo.addr(d, core)
        return RemoteDMATransfer(dst_ids=[DstId(rid=rid, pnc=pid)], dma_engine_mask=mask, remote_sem=handle[rsem],
                                 src=src, dst=dst)

    def issue(transfers, lsem):
        g.remote_dma_fused([t for t, _ in transfers], local_sem=handle[lsem])
        cnt[lsem] += sum(n for _, n in transfers)

    def chip(k, rsem):
        out = []
        for n, p in enumerate(others):
            mask, e = ((1 << (8 + n)), 1) if gateway else ((3 << (2 * n)), 2)
            out.append((transfer(mine[p], mask, rsem, slot(SEND_FROM[gateway][k], side * 8 + p),
                                 slot(RECEIVE_IN[is_gw(p)][k], rank)), e))
        return out

    def cross(k, source, src_of, rsem):
        return [(transfer(theirs[d], 1 << d, rsem, src_of(d), slot(RECEIVE_IN[is_gw(d)][k], side * 8 + source)), 1)
                for d in range(8)]

    CHIP_IN = sum(1 if is_gw(p) else 2 for p in others)
    DIRECT_IN = CHIP_IN + 4
    ROUND_IN = DIRECT_IN + 4
    xlo = (1 - side) * 128
    own = slice(rank * BLK, (rank + 1) * BLK)

    def load(k):
        local(buf[:, SEND_FROM[gateway][k], :], T.x[k])

    def store(k):
        local(T.y[k], buf[:, RECEIVE_IN[gateway][k], :])

    local(slot(RECEIVE_IN[gateway][0], rank), T.x[0][:, own])
    load(0)

    if gateway:
        leaf = [j for j in range(8) if not is_gw(j) and gw_of(j) == me][0]

        def mine_of(k):
            return lambda d: slot(SEND_FROM[True][k], (1 - side) * 8 + d)

        def held(k):
            return lambda d: slot(2, (k % 2) * 8 + d)

        wait("dma")
        issue(cross(0, me, mine_of(0), "a") + chip(0, "a"), "c")
        wait("c", 8 + 8)
        issue(cross(0, leaf, held(0), "a"), "a")
        wait("a", ROUND_IN)
        store(0)
        wait("dma")
        load(1)
        wait("dma")
        issue(cross(1, me, mine_of(1), "b") + chip(1, "b"), "b")
        issue(cross(1, leaf, held(1), "b"), "b")
        wait("b", ROUND_IN)
        store(1)
        wait("dma")
        load(2)
        wait("dma")
        issue(cross(2, me, mine_of(2), "c") + chip(2, "c"), "c")
        wait("c", 16 + DIRECT_IN)
        issue(cross(2, leaf, held(2), "a"), "a")
        wait("a", 4 + 16)
        store(2)
        wait("dma")
        load(3)
        wait("dma")
        issue(cross(3, me, mine_of(3), "b") + chip(3, "b"), "b")
        issue(cross(3, leaf, held(3), "b"), "b")
        wait("b", ROUND_IN)
    else:
        gw = mine[gw_of(me)]

        def hand_over(k, mask, n, rsem):
            return [(transfer(gw, mask, rsem, buf[:, SEND_FROM[False][k], xlo:xlo + 128],
                              buf[:, 2, (k % 2) * 128:(k % 2) * 128 + 128]), n)]

        load(1)
        wait("dma")
        issue(chip(0, "a"), "a")
        issue(hand_over(0, 0x00FF, 8, "c") + hand_over(1, 0xFF00, 8, "c"), "a")
        wait("a", ROUND_IN)
        issue(chip(1, "b"), "b")
        store(0)
        wait("dma")
        load(2)
        wait("b", ROUND_IN)
        wait("dma")
        issue(chip(2, "c"), "c")
        issue(hand_over(2, 0xFFFF, 16, "c"), "c")
        store(1)
        wait("dma")
        load(3)
        wait("c", DIRECT_IN)
        wait("dma")
        issue(hand_over(3, 0xFFFF, 16, "a"), "a")
        issue(chip(3, "b"), "a")
        wait("a", 4)
        store(2)
        wait("b", ROUND_IN)

    store(3)
    wait("dma")
    local(T.y[1:4, :, own], T.x[1:4, :, own])
    wait("dma")
